import numpy as np
import ml_dtypes

BF16 = ml_dtypes.bfloat16


def bf(x):
    return np.asarray(x, np.float32).astype(BF16)


def f32(x):
    return np.asarray(x, np.float32)


def f64(x):
    return np.asarray(x).astype(np.float64)


def striped(idx):
    return np.tile(idx.reshape(-1, 16).T, (8, 1))


S, K, M, N, D, V = 2048, 256, 256, 1536, 4, 384


def setup_inputs():
    return {"table": bf(np.random.standard_normal((K, S))), "w": bf(np.random.standard_normal((D, K, M)) / np.sqrt(D * K)), "b": f32(0.5 * np.random.standard_normal((M, 1))), "offs": striped(np.random.permutation(np.tile(np.arange(S), 2))[:N])}


def reference(table, w, b, offs):
    idx = offs[:16].T.reshape(-1)
    x = f64(table)[:, idx]
    y = sum(f64(w)[t].T @ x[:, t * V : (t + 1) * V] for t in range(D))
    return np.tanh(y + f64(b))

@@ -1,0 +1,57 @@
+import concourse.mybir as mybir
+
+BF16, F32, U16 = mybir.dt.bfloat16, mybir.dt.float32, mybir.dt.uint16
+TANH = mybir.ActivationFunctionType.Tanh
+
+P = 128
+NODES = 2048
+FEATURES_IN = 256
+FEATURES_OUT = 256
+RELATIONS = 4
+PIECE = 384
+PIECE_COLUMNS = PIECE // 16
+K_BLOCKS = FEATURES_IN // P
+M_BLOCKS = FEATURES_OUT // P
+
+FLOPS = 2 * FEATURES_IN * FEATURES_OUT * RELATIONS * PIECE
+
+
+def tile_gather_matmul_kernel(tc, table, w, b, offs, out):
+    nc = tc.nc
+    with (
+        tc.tile_pool(name="held", bufs=1) as held,
+        tc.psum_pool(name="psum", bufs=1) as psum,
+    ):
+        offsets = held.tile([P, RELATIONS * PIECE_COLUMNS], U16, name="offsets")
+        nc.sync.dma_start(offsets[:], offs)
+
+        table_block = [held.tile([P, NODES], BF16, name="table%d" % kb) for kb in range(K_BLOCKS)]
+        weight_block = [
+            held.tile([P, RELATIONS, FEATURES_OUT], BF16, name="weights%d" % kb) for kb in range(K_BLOCKS)
+        ]
+        for kb in range(K_BLOCKS):
+            rows = slice(kb * P, (kb + 1) * P)
+            nc.sync.dma_start(table_block[kb][:], table[rows, :])
+            nc.scalar.dma_start(weight_block[kb][:], w[:, rows, :].rearrange("t p m -> p t m"))
+
+        bias = held.tile([P, M_BLOCKS], F32, name="bias")
+        with nc.allow_non_contiguous_dma(reason="256 single values, one to a partition and column"):
+            nc.scalar.dma_start(bias[:], b.rearrange("(a p) o -> p (a o)", p=P))
+
+        bank = [psum.tile([P, PIECE], F32, name="bank%d" % mb) for mb in range(M_BLOCKS)]
+        for kb in range(K_BLOCKS):
+            for mb in range(M_BLOCKS):
+                for t in range(RELATIONS):
+                    piece = offsets[:, t * PIECE_COLUMNS : (t + 1) * PIECE_COLUMNS]
+                    nc.tensor.matmul(
+                        bank[mb][:],
+                        weight_block[kb][:, t, mb * P : (mb + 1) * P],
+                        table_block[kb][:].indirect(piece),
+                        start=(kb == 0 and t == 0),
+                        stop=(kb == K_BLOCKS - 1 and t == RELATIONS - 1),
+                    )
+
+        for mb in range(M_BLOCKS):
+            result = held.tile([P, PIECE], F32, name="result%d" % mb)
+            nc.scalar.activation(result[:], bank[mb][:], TANH, bias=bias[:, mb : mb + 1])
+            nc.sync.dma_start(out[mb * P : (mb + 1) * P, :], result[:])

@@ -26,17 +26,25 @@ def tile_gather_matmul_kernel(tc, table, w, b, offs, out):
         nc.sync.dma_start(offsets[:], offs)
 
         table_block = [held.tile([P, NODES], BF16, name="table%d" % kb) for kb in range(K_BLOCKS)]
-        weight_block = [
-            held.tile([P, RELATIONS, FEATURES_OUT], BF16, name="weights%d" % kb) for kb in range(K_BLOCKS)
+        weights = [
+            [held.tile([P, FEATURES_OUT], BF16, name="weights%d_%d" % (kb, t)) for t in range(RELATIONS)]
+            for kb in range(K_BLOCKS)
         ]
         for kb in range(K_BLOCKS):
             rows = slice(kb * P, (kb + 1) * P)
             nc.sync.dma_start(table_block[kb][:], table[rows, :])
-            nc.scalar.dma_start(weight_block[kb][:], w[:, rows, :].rearrange("t p m -> p t m"))
+            for t in range(RELATIONS):
+                nc.sync.dma_start(weights[kb][t][:], w[t, rows, :])
 
         bias = held.tile([P, M_BLOCKS], F32, name="bias")
         with nc.allow_non_contiguous_dma(reason="256 single values, one to a partition and column"):
             nc.scalar.dma_start(bias[:], b.rearrange("(a p) o -> p (a o)", p=P))
+
+        zeros = held.tile([P, 128], BF16, name="zeros")
+        nc.vector.memset(zeros[:], 0.0)
+        unread = psum.tile([P, 128], F32, name="unread")
+        for i in range(24):
+            nc.tensor.matmul(unread[:], zeros[:, 0:P], zeros[:], start=True, stop=True)
 
         bank = [psum.tile([P, PIECE], F32, name="bank%d" % mb) for mb in range(M_BLOCKS)]
         for kb in range(K_BLOCKS):
@@ -45,7 +53,7 @@ def tile_gather_matmul_kernel(tc, table, w, b, offs, out):
                     piece = offsets[:, t * PIECE_COLUMNS : (t + 1) * PIECE_COLUMNS]
                     nc.tensor.matmul(
                         bank[mb][:],
-                        weight_block[kb][:, t, mb * P : (mb + 1) * P],
+                        weights[kb][t][:, mb * P : (mb + 1) * P],
                         table_block[kb][:].indirect(piece),
                         start=(kb == 0 and t == 0),
                         stop=(kb == K_BLOCKS - 1 and t == RELATIONS - 1),

@@ -40,12 +40,6 @@ def tile_gather_matmul_kernel(tc, table, w, b, offs, out):
         with nc.allow_non_contiguous_dma(reason="256 single values, one to a partition and column"):
             nc.scalar.dma_start(bias[:], b.rearrange("(a p) o -> p (a o)", p=P))
 
-        zeros = held.tile([P, 128], BF16, name="zeros")
-        nc.vector.memset(zeros[:], 0.0)
-        unread = psum.tile([P, 128], F32, name="unread")
-        for i in range(24):
-            nc.tensor.matmul(unread[:], zeros[:, 0:P], zeros[:], start=True, stop=True)
-
         bank = [psum.tile([P, PIECE], F32, name="bank%d" % mb) for mb in range(M_BLOCKS)]
         for kb in range(K_BLOCKS):
             for mb in range(M_BLOCKS):

@@ -32,9 +32,10 @@ def tile_gather_matmul_kernel(tc, table, w, b, offs, out):
         ]
         for kb in range(K_BLOCKS):
             rows = slice(kb * P, (kb + 1) * P)
-            nc.sync.dma_start(table_block[kb][:], table[rows, :])
+            nc.scalar.dma_start(table_block[kb][:], table[rows, :])
             for t in range(RELATIONS):
-                nc.sync.dma_start(weights[kb][t][:], w[t, rows, :])
+                queue = nc.sync if (kb == 0 and t == 0) else nc.scalar
+                queue.dma_start(weights[kb][t][:], w[t, rows, :])
 
         bias = held.tile([P, M_BLOCKS], F32, name="bias")
         with nc.allow_non_contiguous_dma(reason="256 single values, one to a partition and column"):
@@ -55,5 +56,7 @@ def tile_gather_matmul_kernel(tc, table, w, b, offs, out):
 
         for mb in range(M_BLOCKS):
             result = held.tile([P, PIECE], F32, name="result%d" % mb)
-            nc.scalar.activation(result[:], bank[mb][:], TANH, bias=bias[:, mb : mb + 1])
-            nc.sync.dma_start(out[mb * P : (mb + 1) * P, :], result[:])
+            for half in range(2):
+                columns = slice(half * (PIECE // 2), (half + 1) * (PIECE // 2))
+                nc.scalar.activation(result[:, columns], bank[mb][:, columns], TANH, bias=bias[:, mb : mb + 1])
+                nc.sync.dma_start(out[mb * P : (mb + 1) * P, columns], result[:, columns])

@@ -26,33 +26,36 @@ def tile_gather_matmul_kernel(tc, table, w, b, offs, out):
         nc.sync.dma_start(offsets[:], offs)
 
         table_block = [held.tile([P, NODES], BF16, name="table%d" % kb) for kb in range(K_BLOCKS)]
-        weights = [
-            [held.tile([P, FEATURES_OUT], BF16, name="weights%d_%d" % (kb, t)) for t in range(RELATIONS)]
-            for kb in range(K_BLOCKS)
-        ]
-        for kb in range(K_BLOCKS):
-            rows = slice(kb * P, (kb + 1) * P)
-            nc.scalar.dma_start(table_block[kb][:], table[rows, :])
-            for t in range(RELATIONS):
-                queue = nc.sync if (kb == 0 and t == 0) else nc.scalar
-                queue.dma_start(weights[kb][t][:], w[t, rows, :])
+        weights = [held.tile([P, RELATIONS, FEATURES_OUT], BF16, name="weights%d" % kb) for kb in range(K_BLOCKS)]
+        w_by_row = w.rearrange("t k m -> k t m")
+        nc.sync.dma_start(weights[0][:, 0:1, :], w_by_row[0:P, 0:1, :])
+        nc.scalar.dma_start(table_block[0][:], table[0:P, :])
+        nc.scalar.dma_start(weights[0][:, 1:RELATIONS, :], w_by_row[0:P, 1:RELATIONS, :])
+        nc.scalar.dma_start(table_block[1][:], table[P : 2 * P, :])
+        nc.scalar.dma_start(weights[1][:], w_by_row[P : 2 * P, :, :])
 
         bias = held.tile([P, M_BLOCKS], F32, name="bias")
         with nc.allow_non_contiguous_dma(reason="256 single values, one to a partition and column"):
             nc.scalar.dma_start(bias[:], b.rearrange("(a p) o -> p (a o)", p=P))
 
         bank = [psum.tile([P, PIECE], F32, name="bank%d" % mb) for mb in range(M_BLOCKS)]
-        for kb in range(K_BLOCKS):
+
+        def gathered_matmul(kb, mb, t):
+            piece = offsets[:, t * PIECE_COLUMNS : (t + 1) * PIECE_COLUMNS]
+            nc.tensor.matmul(
+                bank[mb][:],
+                weights[kb][:, t, mb * P : (mb + 1) * P],
+                table_block[kb][:].indirect(piece),
+                start=(kb == 0 and t == 0),
+                stop=(kb == K_BLOCKS - 1 and t == RELATIONS - 1),
+            )
+
+        for t in range(RELATIONS):
             for mb in range(M_BLOCKS):
-                for t in range(RELATIONS):
-                    piece = offsets[:, t * PIECE_COLUMNS : (t + 1) * PIECE_COLUMNS]
-                    nc.tensor.matmul(
-                        bank[mb][:],
-                        weights[kb][t][:, mb * P : (mb + 1) * P],
-                        table_block[kb][:].indirect(piece),
-                        start=(kb == 0 and t == 0),
-                        stop=(kb == K_BLOCKS - 1 and t == RELATIONS - 1),
-                    )
+                gathered_matmul(0, mb, t)
+        for mb in range(M_BLOCKS):
+            for t in range(RELATIONS):
+                gathered_matmul(1, mb, t)
 
         for mb in range(M_BLOCKS):
             result = held.tile([P, PIECE], F32, name="result%d" % mb)

@@ -23,20 +23,20 @@ def tile_gather_matmul_kernel(tc, table, w, b, offs, out):
         tc.psum_pool(name="psum", bufs=1) as psum,
     ):
         offsets = held.tile([P, RELATIONS * PIECE_COLUMNS], U16, name="offsets")
-        nc.sync.dma_start(offsets[:], offs)
 
         table_block = [held.tile([P, NODES], BF16, name="table%d" % kb) for kb in range(K_BLOCKS)]
         weights = [held.tile([P, RELATIONS, FEATURES_OUT], BF16, name="weights%d" % kb) for kb in range(K_BLOCKS)]
         w_by_row = w.rearrange("t k m -> k t m")
-        nc.sync.dma_start(weights[0][:, 0:1, :], w_by_row[0:P, 0:1, :])
-        nc.scalar.dma_start(table_block[0][:], table[0:P, :])
-        nc.scalar.dma_start(weights[0][:, 1:RELATIONS, :], w_by_row[0:P, 1:RELATIONS, :])
-        nc.scalar.dma_start(table_block[1][:], table[P : 2 * P, :])
-        nc.scalar.dma_start(weights[1][:], w_by_row[P : 2 * P, :, :])
+        nc.sync.dma_start(table_block[0][:], table[0:P, :])
+        nc.sync.dma_start(offsets[:], offs)
+        nc.scalar.dma_start(weights[0][:, 0:1, :], w_by_row[0:P, 0:1, :])
+        nc.sync.dma_start(weights[0][:, 1:RELATIONS, :], w_by_row[0:P, 1:RELATIONS, :])
+        nc.sync.dma_start(table_block[1][:], table[P : 2 * P, :])
+        nc.sync.dma_start(weights[1][:], w_by_row[P : 2 * P, :, :])
 
         bias = held.tile([P, M_BLOCKS], F32, name="bias")
         with nc.allow_non_contiguous_dma(reason="256 single values, one to a partition and column"):
-            nc.scalar.dma_start(bias[:], b.rearrange("(a p) o -> p (a o)", p=P))
+            nc.sync.dma_start(bias[:], b.rearrange("(a p) o -> p (a o)", p=P))
 
         bank = [psum.tile([P, PIECE], F32, name="bank%d" % mb) for mb in range(M_BLOCKS)]
 

@@ -50,12 +50,10 @@ def tile_gather_matmul_kernel(tc, table, w, b, offs, out):
                 stop=(kb == K_BLOCKS - 1 and t == RELATIONS - 1),
             )
 
-        for t in range(RELATIONS):
+        for kb in range(K_BLOCKS):
             for mb in range(M_BLOCKS):
-                gathered_matmul(0, mb, t)
-        for mb in range(M_BLOCKS):
-            for t in range(RELATIONS):
-                gathered_matmul(1, mb, t)
+                for t in range(RELATIONS):
+                    gathered_matmul(kb, mb, t)
 
         for mb in range(M_BLOCKS):
             result = held.tile([P, PIECE], F32, name="result%d" % mb)

@@ -12,6 +12,7 @@ PIECE = 384
 PIECE_COLUMNS = PIECE // 16
 K_BLOCKS = FEATURES_IN // P
 M_BLOCKS = FEATURES_OUT // P
+TRANSACTION_BYTES = 256
 
 FLOPS = 2 * FEATURES_IN * FEATURES_OUT * RELATIONS * PIECE
 
@@ -24,8 +25,13 @@ def tile_gather_matmul_kernel(tc, table, w, b, offs, out):
     ):
         offsets = held.tile([P, RELATIONS * PIECE_COLUMNS], U16, name="offsets")
 
-        table_block = [held.tile([P, NODES], BF16, name="table%d" % kb) for kb in range(K_BLOCKS)]
-        weights = [held.tile([P, RELATIONS, FEATURES_OUT], BF16, name="weights%d" % kb) for kb in range(K_BLOCKS)]
+        table_block = [
+            held.tile([P, NODES], BF16, name="table%d" % kb, align_bytes=TRANSACTION_BYTES) for kb in range(K_BLOCKS)
+        ]
+        weights = [
+            held.tile([P, RELATIONS, FEATURES_OUT], BF16, name="weights%d" % kb, align_bytes=TRANSACTION_BYTES)
+            for kb in range(K_BLOCKS)
+        ]
         w_by_row = w.rearrange("t k m -> k t m")
         nc.sync.dma_start(table_block[0][:], table[0:P, :])
         nc.sync.dma_start(offsets[:], offs)
@@ -56,7 +62,7 @@ def tile_gather_matmul_kernel(tc, table, w, b, offs, out):
                     gathered_matmul(kb, mb, t)
 
         for mb in range(M_BLOCKS):
-            result = held.tile([P, PIECE], F32, name="result%d" % mb)
+            result = held.tile([P, PIECE], F32, name="result%d" % mb, align_bytes=TRANSACTION_BYTES)
             for half in range(2):
                 columns = slice(half * (PIECE // 2), (half + 1) * (PIECE // 2))
                 nc.scalar.activation(result[:, columns], bank[mb][:, columns], TANH, bias=bias[:, mb : mb + 1])

@@ -13,6 +13,7 @@ PIECE_COLUMNS = PIECE // 16
 K_BLOCKS = FEATURES_IN // P
 M_BLOCKS = FEATURES_OUT // P
 TRANSACTION_BYTES = 256
+STORE_COLUMNS = 128
 
 FLOPS = 2 * FEATURES_IN * FEATURES_OUT * RELATIONS * PIECE
 
@@ -63,7 +64,7 @@ def tile_gather_matmul_kernel(tc, table, w, b, offs, out):
 
         for mb in range(M_BLOCKS):
             result = held.tile([P, PIECE], F32, name="result%d" % mb, align_bytes=TRANSACTION_BYTES)
-            for half in range(2):
-                columns = slice(half * (PIECE // 2), (half + 1) * (PIECE // 2))
+            for first in range(0, PIECE, STORE_COLUMNS):
+                columns = slice(first, first + STORE_COLUMNS)
                 nc.scalar.activation(result[:, columns], bank[mb][:, columns], TANH, bias=bias[:, mb : mb + 1])
                 nc.sync.dma_start(out[mb * P : (mb + 1) * P, columns], result[:, columns])

import concourse.mybir as mybir

BF16, F32, U16 = mybir.dt.bfloat16, mybir.dt.float32, mybir.dt.uint16
TANH = mybir.ActivationFunctionType.Tanh

P = 128
NODES = 2048
FEATURES_IN = 256
FEATURES_OUT = 256
RELATIONS = 4
PIECE = 384
PIECE_COLUMNS = PIECE // 16
K_BLOCKS = FEATURES_IN // P
M_BLOCKS = FEATURES_OUT // P
TRANSACTION_BYTES = 256
STORE_COLUMNS = 128

FLOPS = 2 * FEATURES_IN * FEATURES_OUT * RELATIONS * PIECE


def tile_gather_matmul_kernel(tc, table, w, b, offs, out):
    nc = tc.nc
    with (
        tc.tile_pool(name="held", bufs=1) as held,
        tc.psum_pool(name="psum", bufs=1) as psum,
    ):
        offsets = held.tile([P, RELATIONS * PIECE_COLUMNS], U16, name="offsets")

        table_block = [
            held.tile([P, NODES], BF16, name="table%d" % kb, align_bytes=TRANSACTION_BYTES) for kb in range(K_BLOCKS)
        ]
        weights = [
            held.tile([P, RELATIONS, FEATURES_OUT], BF16, name="weights%d" % kb, align_bytes=TRANSACTION_BYTES)
            for kb in range(K_BLOCKS)
        ]
        w_by_row = w.rearrange("t k m -> k t m")
        nc.sync.dma_start(table_block[0][:], table[0:P, :])
        nc.sync.dma_start(offsets[:], offs)
        nc.scalar.dma_start(weights[0][:, 0:1, :], w_by_row[0:P, 0:1, :])
        nc.sync.dma_start(weights[0][:, 1:RELATIONS, :], w_by_row[0:P, 1:RELATIONS, :])
        nc.sync.dma_start(table_block[1][:], table[P : 2 * P, :])
        nc.sync.dma_start(weights[1][:], w_by_row[P : 2 * P, :, :])

        bias = held.tile([P, M_BLOCKS], F32, name="bias")
        with nc.allow_non_contiguous_dma(reason="256 single values, one to a partition and column"):
            nc.sync.dma_start(bias[:], b.rearrange("(a p) o -> p (a o)", p=P))

        bank = [psum.tile([P, PIECE], F32, name="bank%d" % mb) for mb in range(M_BLOCKS)]

        def gathered_matmul(kb, mb, t):
            piece = offsets[:, t * PIECE_COLUMNS : (t + 1) * PIECE_COLUMNS]
            nc.tensor.matmul(
                bank[mb][:],
                weights[kb][:, t, mb * P : (mb + 1) * P],
                table_block[kb][:].indirect(piece),
                start=(kb == 0 and t == 0),
                stop=(kb == K_BLOCKS - 1 and t == RELATIONS - 1),
            )

        for kb in range(K_BLOCKS):
            for mb in range(M_BLOCKS):
                for t in range(RELATIONS):
                    gathered_matmul(kb, mb, t)

        for mb in range(M_BLOCKS):
            result = held.tile([P, PIECE], F32, name="result%d" % mb, align_bytes=TRANSACTION_BYTES)
            for first in range(0, PIECE, STORE_COLUMNS):
                columns = slice(first, first + STORE_COLUMNS)
                nc.scalar.activation(result[:, columns], bank[mb][:, columns], TANH, bias=bias[:, mb : mb + 1])
                nc.sync.dma_start(out[mb * P : (mb + 1) * P, columns], result[:, columns])
